import numpy as np
import ml_dtypes


def mxq(x, axis, fmt="e4m3"):
    dtype, down = {"e4m3": (ml_dtypes.float8_e4m3fn, 7), "e5m2": (ml_dtypes.float8_e5m2, 14)}[fmt]
    v = np.moveaxis(np.asarray(x, np.float32).astype(ml_dtypes.bfloat16).astype(np.float64), axis, -1)
    blocks = v.reshape(v.shape[:-1] + (-1, 32))
    amax = np.abs(blocks).max(-1, keepdims=True)
    byte = np.maximum(np.where(amax > 0, np.frexp(amax)[1] - 1 + 127, 0) - down, 1)
    scale = np.exp2(byte - 127.0)
    codes = (blocks / scale).astype(np.float32).astype(dtype).astype(np.float64)
    return np.moveaxis((codes * scale).reshape(v.shape), -1, axis)


WIDE = False


def mx_kscale(k):
    if not WIDE:
        return np.ones(k)
    levels = np.array([10, -10, 5, -5, 0])
    if k % 512:
        return np.exp2(np.random.permutation(np.resize(levels, k // 32))).repeat(32)
    a = np.empty((k // 512, 16))
    for p in range(k // 512):
        a[p, :8] = np.random.permutation(np.resize(levels, 8))
        for g in range(8):
            far = levels[np.abs(levels - a[p, g]) >= 10]
            a[p, g + 8] = far[np.random.randint(len(far))]
    return np.exp2(a.ravel()).repeat(32)


def f64(x):
    return np.asarray(x).astype(np.float64)


def striped(idx):
    return np.tile(idx.reshape(-1, 16).T, (8, 1)).astype(np.uint16)


def unstriped(offs):
    return offs[:16].T.reshape(-1).astype(np.int64)


def striped8(idx):
    return np.concatenate([x.reshape(-1, 16).T for x in idx]).astype(np.uint16)


def runs(offs, k):
    lists = np.stack([offs[16 * r : 16 * r + 16].T.reshape(-1) for r in range(8)]).astype(np.int64)
    return lists[np.arange(k) % 512 // 64]


def pack_weight(w):
    k, n = w.shape
    w = f64(np.asarray(w, np.float32).astype(ml_dtypes.bfloat16)).reshape(k // 32, 32, n)
    amax = np.abs(w).max(1)
    byte = np.clip(np.where(amax > 0, np.frexp(amax)[1] - 1 + 127 - 7, 1), 1, 254)
    scaled = (w * np.exp2(127.0 - byte)[:, None, :]).reshape(k, n).astype(np.float32)
    words = np.ascontiguousarray(scaled.reshape(k // 512, 128, 4, n).transpose(0, 1, 3, 2)).astype(ml_dtypes.float8_e4m3fn).view(np.uint8)
    return words, np.ascontiguousarray(byte.astype(np.uint8).reshape(k // 512, 16, n))


def unpack_weight(words, scales):
    g, p, n, _ = words.shape
    vals = np.ascontiguousarray(words).view(ml_dtypes.float8_e4m3fn).astype(np.float64) * np.repeat(np.exp2(scales.astype(np.float64) - 127.0), 8, axis=1)[..., None]
    return vals.transpose(0, 1, 3, 2).reshape(g * 512, n)


K, T, S, N, H, W = 512, 2048, 512, 512, 512, 256


def setup_inputs():
    n = np.random.standard_normal
    s = mx_kscale(K)[:, None]
    u = mx_kscale(H)
    packed_xT = pack_weight(n((K, T)) * s)
    perm = np.stack([np.random.permutation(S) for _ in range(8)])
    return {
        "x_words": packed_xT[0],
        "x_scales": packed_xT[1],
        "w1": (n((K, H)) / np.sqrt(K) / s).astype(np.float32),
        "gn": (np.random.uniform(0.5, 1.5, (H, 1)) * u[:, None]).astype(np.float32),
        "w2": (n((H, N)) / np.sqrt(H) / u[:, None]).astype(np.float32),
        "gm": (np.random.uniform(0.5, 1.5, (H, 1)) * u[:, None]).astype(np.float32),
        "w3": (n((H, N)) / np.sqrt(H) / u[:, None]).astype(np.float32),
        "offs": striped(np.random.permutation(T)[:S]),
        "n1": striped8(np.stack([np.random.permutation(S) for _ in range(8)])),
        "n2": striped8(np.stack([np.random.permutation(S) for _ in range(8)])),
        "n3": striped8(perm[:, :W]),
        "n4": striped8(perm[:, W:]),
        "n5": striped8(np.stack([np.random.permutation(S) for _ in range(8)])),
        "n6": striped8(np.stack([np.random.permutation(S) for _ in range(8)])),
        "n7": striped8(np.stack([np.random.permutation(S) for _ in range(8)])),
    }


def reference(x_words, x_scales, w1, gn, w2, gm, w3, offs, n1, n2, n3, n4, n5, n6, n7):
    xq = unpack_weight(x_words, x_scales)[:, unstriped(offs)]
    y = mxq(f64(w1), 0, "e4m3").T @ xq
    st = y + 0.5 * (y[np.arange(H)[:, None], runs(n1, H)])
    z = f64(gn) * (st - (st[np.arange(H)[:, None], runs(n2, H)]))
    a = mxq(f64(w2), 0, "e4m3").T @ mxq(z, 0, "e4m3")
    pa = y[np.arange(H)[:, None], runs(n3, H)]
    pb = y[np.arange(H)[:, None], runs(n4, H)]
    rb = pa * pb
    ra = pa + pb
    ds = np.zeros((H, S))
    ds[np.arange(H)[:, None], runs(n3, H)] = ra
    dt = ds.copy()
    dt[np.arange(H)[:, None], runs(n4, H)] = rb
    z2 = f64(gm) * dt
    b = mxq(f64(w3), 0, "e4m3").T @ mxq(z2, 0, "e4m3")
    return np.maximum(np.minimum(a - (0.5 * (a[np.arange(N)[:, None], runs(n5, N)])), b[np.arange(N)[:, None], runs(n6, N)]), b[np.arange(N)[:, None], runs(n7, N)])

@@ -1,0 +1,195 @@
+from contextlib import ExitStack
+
+import concourse.mybir as mybir
+
+K, T, S, N, H, W = 512, 2048, 512, 512, 512, 256
+FLOPS = 2 * S * (K * H + 2 * H * N)
+
+F32 = mybir.dt.float32
+BF16 = mybir.dt.bfloat16
+I32 = mybir.dt.int32
+U32 = mybir.dt.uint32
+U16 = mybir.dt.uint16
+U8 = mybir.dt.uint8
+FP8X4 = mybir.dt.float8_e4m3fn_x4
+ALU = mybir.AluOpType
+COPY = mybir.ActivationFunctionType.Copy
+
+P = 128
+PACK = 4
+SCALAR_SHARE = 40
+
+
+def tile_picked_forkclampbhopbond_none_p_kernel(
+    tc, x_words, x_scales, w1, gn, w2, gm, w3, offs, n1, n2, n3, n4, n5, n6, n7, out
+):
+    nc = tc.nc
+    tiles = range(PACK)
+
+    with ExitStack() as ctx:
+        keep = ctx.enter_context(tc.tile_pool(name="keep", bufs=1))
+        psum = ctx.enter_context(tc.psum_pool(name="psum", bufs=1))
+
+        def load_list(src, name):
+            dst = keep.tile(list(src.shape), U16, name=name)
+            nc.sync.dma_start(dst[:], src)
+            return dst
+
+        def load_weight(src, name):
+            dst = keep.tile([P, PACK, src.shape[1]], F32, name=name)
+            nc.sync.dma_start(dst[:], src.rearrange("(p j) c -> p j c", j=PACK))
+            return dst
+
+        def load_gain(src, name):
+            dst = keep.tile([P, PACK], F32, name=name)
+            nc.sync.dma_start(dst[:], src.rearrange("(p t) o -> p (t o)", t=PACK))
+            return dst
+
+        def dealt_views(raw, name):
+            grouped = keep.tile([P, PACK, P, PACK], BF16, name=name, align_bytes=64)
+            return grouped, grouped[:].rearrange("p t m j -> p m j t"), raw[:].rearrange("p j (m t) -> p m j t", t=PACK)
+
+        def quantize(flat, name):
+            codes = keep.tile([P, flat.shape[1] // PACK], U32, name=name + "_codes", align_bytes=64)
+            scales = keep.tile([P, flat.shape[1] // PACK], U8, name=name + "_scales", align_bytes=64)
+            nc.vector.quantize_mx(out=codes[:].bitcast(FP8X4), scales=scales[:], in_=flat)
+            return codes, scales
+
+        def product(weight, moving, t, bank):
+            acc = psum.tile([P, S], F32, name="acc", tag="bank%d" % bank)
+            cols = slice(t * P, (t + 1) * P)
+            nc.tensor.matmul_mx(
+                out=acc[:],
+                lhsT=weight[0][:, cols].bitcast(FP8X4),
+                lhsT_scale=weight[1][:, cols],
+                rhs=moving[0][:].bitcast(FP8X4),
+                rhs_scale=moving[1][:],
+                start=True,
+                stop=True,
+            )
+            return acc
+
+        def rows(name, width=S):
+            return [keep.tile([P, width], F32, name="%s%d" % (name, t)) for t in tiles]
+
+        table_scales = keep.tile([P, T], U8, name="table_scales")
+        nc.vector.memset(table_scales[:].bitcast(I32), 0)
+        offs_sb = load_list(offs, "offs_sb")
+        w1_raw = load_weight(w1, "w1_raw")
+        for q in range(4):
+            nc.sync.dma_start(
+                table_scales[32 * q : 32 * q + 4, :].bitcast(I32),
+                x_scales[0, 4 * q : 4 * q + 4, :].bitcast(I32),
+            )
+        table_words = keep.tile([P, T], U32, name="table_words")
+        nc.sync.dma_start(table_words[:].bitcast(I32), x_words[0].rearrange("p n t -> p (n t)").bitcast(I32))
+        n3_sb = load_list(n3, "n3_sb")
+        n4_sb = load_list(n4, "n4_sb")
+        gm_sb = load_gain(gm, "gm_sb")
+        gn_sb = load_gain(gn, "gn_sb")
+        w3_raw = load_weight(w3, "w3_raw")
+        n1_sb = load_list(n1, "n1_sb")
+        n2_sb = load_list(n2, "n2_sb")
+        w2_raw = load_weight(w2, "w2_raw")
+        n6_sb = load_list(n6, "n6_sb")
+        n7_sb = load_list(n7, "n7_sb")
+        n5_sb = load_list(n5, "n5_sb")
+
+        x_scale_g = keep.tile([P, S], U8, name="x_scale_g", align_bytes=64)
+        nc.vector.tensor_copy(x_scale_g[:], table_scales[:].indirect(offs_sb[:]))
+        w1_g, dst, src = dealt_views(w1_raw, "w1_g")
+        nc.scalar.activation(dst[:, :SCALAR_SHARE], src[:, :SCALAR_SHARE], COPY)
+        nc.vector.tensor_copy(dst[:, SCALAR_SHARE:], src[:, SCALAR_SHARE:])
+        w1_q = quantize(w1_g[:].rearrange("p t m j -> p (t m j)"), "w1")
+        x_word_g = keep.tile([P, S], U32, name="x_word_g", align_bytes=64)
+        nc.vector.tensor_copy(x_word_g[:], table_words[:].indirect(offs_sb[:]))
+        y_acc = [product(w1_q, (x_word_g, x_scale_g), t, t) for t in tiles]
+        y = rows("y")
+        for t in tiles:
+            nc.scalar.activation(y[t][:], y_acc[t][:], COPY)
+
+        pa, pb, dt = rows("pa", W), rows("pb", W), rows("dt")
+        z2_g = keep.tile([P, S, PACK], BF16, name="z2_g", align_bytes=64)
+        gy, gy2 = rows("gy", 2 * S), rows("gy2")
+
+        def fetch_pair(t):
+            nc.vector.tensor_copy(pa[t][:], y[t][:].indirect(n3_sb[:]))
+            nc.vector.tensor_copy(pb[t][:], y[t][:].indirect(n4_sb[:]))
+
+        def put(t, places, op):
+            nc.vector.tensor_tensor(dt[t][:].indirect(places[:]), pa[t][:], pb[t][:], op)
+
+        w3_g, dst3, src3 = dealt_views(w3_raw, "w3_g")
+        w2_g, dst2, src2 = dealt_views(w2_raw, "w2_g")
+        for t in range(0, PACK, 2):
+            fetch_pair(t)
+            fetch_pair(t + 1)
+            put(t, n3_sb, ALU.add)
+            put(t + 1, n3_sb, ALU.add)
+            put(t, n4_sb, ALU.mult)
+            put(t + 1, n4_sb, ALU.mult)
+            if t == 0:
+                nc.scalar.activation(dst3, src3, COPY)
+                w3_q = quantize(w3_g[:].rearrange("p t m j -> p (t m j)"), "w3")
+                for u in tiles:
+                    nc.scalar.activation(gy[u][:, :S], y_acc[u][:], COPY, scale=gn_sb[:, u : u + 1])
+                    nc.scalar.activation(gy2[u][:], gy[u][:, :S], COPY, scale=2.0)
+            for u in (t, t + 1):
+                nc.scalar.activation(z2_g[:, :, u], dt[u][:], COPY, scale=gm_sb[:, u : u + 1])
+            if t == 0:
+                nc.scalar.activation(dst2, src2, COPY)
+
+        st, st_plain = rows("st", 2 * S), rows("st_plain")
+        z = keep.tile([P, PACK, S], F32, name="z")
+        for t in tiles:
+            nc.vector.tensor_tensor(st[t][:, :S], gy[t][:].indirect(n1_sb[:]), gy2[t][:], ALU.add)
+            nc.scalar.activation(st_plain[t][:], st[t][:, :S], COPY)
+        z2_q = quantize(z2_g[:].rearrange("p s t -> p (s t)"), "z2")
+        b_acc = [product(w3_q, z2_q, t, PACK + t) for t in tiles]
+        b = rows("b", 2 * S)
+        for t in tiles:
+            nc.scalar.activation(b[t][:, :S], b_acc[t][:], COPY)
+        for t in tiles:
+            nc.vector.tensor_tensor(z[:, t, :], st[t][:].indirect(n2_sb[:]), st_plain[t][:], ALU.subtract)
+        w2_q = quantize(w2_g[:].rearrange("p t m j -> p (t m j)"), "w2")
+        z_g = keep.tile([P, S, PACK], BF16, name="z_g", align_bytes=64)
+        nc.scalar.activation(
+            z_g[:].rearrange("p (c i) t -> p c t i", i=4),
+            z[:].rearrange("p t (c i) -> p c t i", i=4),
+            COPY,
+            scale=-0.5,
+        )
+
+        b6, b7 = rows("b6"), rows("b7")
+
+        def fetch_b(t):
+            nc.vector.tensor_copy(b6[t][:], b[t][:].indirect(n6_sb[:]))
+            nc.vector.tensor_copy(b7[t][:], b[t][:].indirect(n7_sb[:]))
+
+        fetch_b(0)
+        fetch_b(1)
+        z_q = quantize(z_g[:].rearrange("p s t -> p (s t)"), "z")
+        a_acc = [product(w2_q, z_q, t, t) for t in tiles]
+        a_half, a = rows("a_half", 2 * S), rows("a")
+        for t in tiles:
+            nc.scalar.activation(a_half[t][:, :S], a_acc[t][:], COPY, scale=-0.5)
+            nc.scalar.activation(a[t][:], a_acc[t][:], COPY)
+        fetch_b(2)
+        fetch_b(3)
+        hop, low, res = rows("hop"), rows("low"), rows("res")
+        out_rows = out.rearrange("(p t) j -> p t j", t=PACK)
+
+        def finish_low(t):
+            nc.vector.tensor_tensor(low[t][:], hop[t][:], b6[t][:], ALU.min)
+
+        def finish_out(t):
+            nc.vector.tensor_tensor(res[t][:], low[t][:], b7[t][:], ALU.max)
+            nc.sync.dma_start(out_rows[:, t, :], res[t][:])
+
+        for step in range(PACK + 2):
+            if step < PACK:
+                nc.vector.tensor_tensor(hop[step][:], a_half[step][:].indirect(n5_sb[:]), a[step][:], ALU.add)
+            if 0 <= step - 1 < PACK:
+                finish_low(step - 1)
+            if 0 <= step - 2 < PACK:
+                finish_out(step - 2)

@@ -1,6 +1,7 @@
 from contextlib import ExitStack
 
 import concourse.mybir as mybir
+from concourse.masks import make_identity
 
 K, T, S, N, H, W = 512, 2048, 512, 512, 512, 256
 FLOPS = 2 * S * (K * H + 2 * H * N)
@@ -17,7 +18,7 @@ COPY = mybir.ActivationFunctionType.Copy
 
 P = 128
 PACK = 4
-SCALAR_SHARE = 40
+SCALAR_SHARE = 52
 
 
 def tile_picked_forkclampbhopbond_none_p_kernel(
@@ -55,22 +56,25 @@ def tile_picked_forkclampbhopbond_none_p_kernel(
             nc.vector.quantize_mx(out=codes[:].bitcast(FP8X4), scales=scales[:], in_=flat)
             return codes, scales
 
-        def product(weight, moving, t, bank):
-            acc = psum.tile([P, S], F32, name="acc", tag="bank%d" % bank)
+        def product(weight, moving, t, bank, places=slice(0, S)):
+            acc = psum.tile([P, places.stop - places.start], F32, name="acc", tag="bank%d" % bank)
             cols = slice(t * P, (t + 1) * P)
             nc.tensor.matmul_mx(
                 out=acc[:],
                 lhsT=weight[0][:, cols].bitcast(FP8X4),
                 lhsT_scale=weight[1][:, cols],
-                rhs=moving[0][:].bitcast(FP8X4),
-                rhs_scale=moving[1][:],
+                rhs=moving[0][:, places].bitcast(FP8X4),
+                rhs_scale=moving[1][:, places],
                 start=True,
                 stop=True,
             )
             return acc
 
+        def row(name, width=S, tag=None, bufs=1):
+            return keep.tile([P, width], F32, name=name, tag=tag or name, bufs=bufs, align_bytes=64)
+
         def rows(name, width=S):
-            return [keep.tile([P, width], F32, name="%s%d" % (name, t)) for t in tiles]
+            return [row("%s%d" % (name, t), width) for t in tiles]
 
         table_scales = keep.tile([P, T], U8, name="table_scales")
         nc.vector.memset(table_scales[:].bitcast(I32), 0)
@@ -85,15 +89,20 @@ def tile_picked_forkclampbhopbond_none_p_kernel(
         nc.sync.dma_start(table_words[:].bitcast(I32), x_words[0].rearrange("p n t -> p (n t)").bitcast(I32))
         n3_sb = load_list(n3, "n3_sb")
         n4_sb = load_list(n4, "n4_sb")
-        gm_sb = load_gain(gm, "gm_sb")
         gn_sb = load_gain(gn, "gn_sb")
-        w3_raw = load_weight(w3, "w3_raw")
         n1_sb = load_list(n1, "n1_sb")
         n2_sb = load_list(n2, "n2_sb")
         w2_raw = load_weight(w2, "w2_raw")
+        w3_raw = load_weight(w3, "w3_raw")
+        gm_sb = load_gain(gm, "gm_sb")
+        n5_sb = load_list(n5, "n5_sb")
         n6_sb = load_list(n6, "n6_sb")
         n7_sb = load_list(n7, "n7_sb")
-        n5_sb = load_list(n5, "n5_sb")
+        identity = keep.tile([P, P], F32, name="identity")
+        make_identity(nc, identity[:])
+
+        halves = [slice(0, S // 2), slice(S // 2, S)]
+        list_halves = [slice(0, S // 32), slice(S // 32, S // 16)]
 
         x_scale_g = keep.tile([P, S], U8, name="x_scale_g", align_bytes=64)
         nc.vector.tensor_copy(x_scale_g[:], table_scales[:].indirect(offs_sb[:]))
@@ -101,57 +110,38 @@ def tile_picked_forkclampbhopbond_none_p_kernel(
         nc.scalar.activation(dst[:, :SCALAR_SHARE], src[:, :SCALAR_SHARE], COPY)
         nc.vector.tensor_copy(dst[:, SCALAR_SHARE:], src[:, SCALAR_SHARE:])
         w1_q = quantize(w1_g[:].rearrange("p t m j -> p (t m j)"), "w1")
-        x_word_g = keep.tile([P, S], U32, name="x_word_g", align_bytes=64)
-        nc.vector.tensor_copy(x_word_g[:], table_words[:].indirect(offs_sb[:]))
-        y_acc = [product(w1_q, (x_word_g, x_scale_g), t, t) for t in tiles]
+        x_word_g = keep.tile([P, S], U32, name="x_word_g", tag="w1_g", align_bytes=64)
+        for h in range(2):
+            nc.vector.tensor_copy(x_word_g[:, halves[h]], table_words[:].indirect(offs_sb[:, list_halves[h]]))
+        x_q = (x_word_g, x_scale_g)
+        y_acc = [[(halves[h], product(w1_q, x_q, 0, PACK * h, halves[h])) for h in range(2)]]
+        y_acc.extend([(slice(0, S), product(w1_q, x_q, t, t))] for t in range(1, PACK))
         y = rows("y")
         for t in tiles:
-            nc.scalar.activation(y[t][:], y_acc[t][:], COPY)
+            for places, acc in y_acc[t]:
+                nc.scalar.activation(y[t][:, places], acc[:], COPY)
 
-        pa, pb, dt = rows("pa", W), rows("pb", W), rows("dt")
-        z2_g = keep.tile([P, S, PACK], BF16, name="z2_g", align_bytes=64)
-        gy, gy2 = rows("gy", 2 * S), rows("gy2")
-
-        def fetch_pair(t):
+        pa, pb = rows("pa", W), rows("pb", W)
+        for t in tiles:
             nc.vector.tensor_copy(pa[t][:], y[t][:].indirect(n3_sb[:]))
             nc.vector.tensor_copy(pb[t][:], y[t][:].indirect(n4_sb[:]))
 
-        def put(t, places, op):
-            nc.vector.tensor_tensor(dt[t][:].indirect(places[:]), pa[t][:], pb[t][:], op)
-
-        w3_g, dst3, src3 = dealt_views(w3_raw, "w3_g")
-        w2_g, dst2, src2 = dealt_views(w2_raw, "w2_g")
-        for t in range(0, PACK, 2):
-            fetch_pair(t)
-            fetch_pair(t + 1)
-            put(t, n3_sb, ALU.add)
-            put(t + 1, n3_sb, ALU.add)
-            put(t, n4_sb, ALU.mult)
-            put(t + 1, n4_sb, ALU.mult)
-            if t == 0:
-                nc.scalar.activation(dst3, src3, COPY)
-                w3_q = quantize(w3_g[:].rearrange("p t m j -> p (t m j)"), "w3")
-                for u in tiles:
-                    nc.scalar.activation(gy[u][:, :S], y_acc[u][:], COPY, scale=gn_sb[:, u : u + 1])
-                    nc.scalar.activation(gy2[u][:], gy[u][:, :S], COPY, scale=2.0)
-            for u in (t, t + 1):
-                nc.scalar.activation(z2_g[:, :, u], dt[u][:], COPY, scale=gm_sb[:, u : u + 1])
-            if t == 0:
-                nc.scalar.activation(dst2, src2, COPY)
-
+        gy, gy2 = rows("gy", 2 * S), rows("gy2")
+        for t in tiles:
+            for places, acc in y_acc[t]:
+                nc.scalar.activation(gy[t][:, places], acc[:], COPY, scale=gn_sb[:, t : t + 1])
+            nc.scalar.activation(gy2[t][:], gy[t][:, :S], COPY, scale=2.0)
         st, st_plain = rows("st", 2 * S), rows("st_plain")
-        z = keep.tile([P, PACK, S], F32, name="z")
+        z = keep.tile([P, PACK, S], F32, name="z", align_bytes=64)
         for t in tiles:
             nc.vector.tensor_tensor(st[t][:, :S], gy[t][:].indirect(n1_sb[:]), gy2[t][:], ALU.add)
             nc.scalar.activation(st_plain[t][:], st[t][:, :S], COPY)
-        z2_q = quantize(z2_g[:].rearrange("p s t -> p (s t)"), "z2")
-        b_acc = [product(w3_q, z2_q, t, PACK + t) for t in tiles]
-        b = rows("b", 2 * S)
-        for t in tiles:
-            nc.scalar.activation(b[t][:, :S], b_acc[t][:], COPY)
         for t in tiles:
             nc.vector.tensor_tensor(z[:, t, :], st[t][:].indirect(n2_sb[:]), st_plain[t][:], ALU.subtract)
-        w2_q = quantize(w2_g[:].rearrange("p t m j -> p (t m j)"), "w2")
+        w2_g, dst, src = dealt_views(w2_raw, "w2_g")
+        nc.scalar.activation(dst, src, COPY)
+        w3_g, dst, src = dealt_views(w3_raw, "w3_g")
+        nc.scalar.activation(dst, src, COPY)
         z_g = keep.tile([P, S, PACK], BF16, name="z_g", align_bytes=64)
         nc.scalar.activation(
             z_g[:].rearrange("p (c i) t -> p c t i", i=4),
@@ -160,36 +150,99 @@ def tile_picked_forkclampbhopbond_none_p_kernel(
             scale=-0.5,
         )
 
-        b6, b7 = rows("b6"), rows("b7")
+        z2_g = keep.tile([P, S, PACK], BF16, name="z2_g", align_bytes=64)
 
-        def fetch_b(t):
-            nc.vector.tensor_copy(b6[t][:], b[t][:].indirect(n6_sb[:]))
-            nc.vector.tensor_copy(b7[t][:], b[t][:].indirect(n7_sb[:]))
+        def put_pairs(first, tags):
+            pair = (first, first + 1)
+            dt = {t: row("dt%d" % t, tag=tag) for t, tag in zip(pair, tags)}
+            for places, op in ((n3_sb, ALU.add), (n4_sb, ALU.mult)):
+                for t in pair:
+                    nc.vector.tensor_tensor(dt[t][:].indirect(places[:]), pa[t][:], pb[t][:], op)
+            for t in pair:
+                nc.scalar.activation(z2_g[:, :, t], dt[t][:], COPY, scale=gm_sb[:, t : t + 1])
 
-        fetch_b(0)
-        fetch_b(1)
+        put_pairs(0, ("st_plain2", "st_plain3"))
+        w2_q = quantize(w2_g[:].rearrange("p t m j -> p (t m j)"), "w2")
+        w3_q = quantize(w3_g[:].rearrange("p t m j -> p (t m j)"), "w3")
         z_q = quantize(z_g[:].rearrange("p s t -> p (s t)"), "z")
         a_acc = [product(w2_q, z_q, t, t) for t in tiles]
         a_half, a = rows("a_half", 2 * S), rows("a")
-        for t in tiles:
+
+        def copy_a(t):
             nc.scalar.activation(a_half[t][:, :S], a_acc[t][:], COPY, scale=-0.5)
             nc.scalar.activation(a[t][:], a_acc[t][:], COPY)
-        fetch_b(2)
-        fetch_b(3)
-        hop, low, res = rows("hop"), rows("low"), rows("res")
+
+        for t in range(PACK - 1):
+            copy_a(t)
+        put_pairs(2, ("z", "z_g"))
+        copy_a(PACK - 1)
+
+        early = keep.tile([P, 2, S], F32, name="hop_early")
+        hop = [early[:, 0, :], early[:, 1, :]]
+
+        def fetch_hop(t):
+            nc.vector.tensor_tensor(hop[t], a_half[t][:].indirect(n5_sb[:]), a[t][:], ALU.add)
+
+        fetch_hop(0)
+        fetch_hop(1)
+        z2_q = quantize(z2_g[:].rearrange("p s t -> p (s t)"), "z2")
+        b_acc = [product(w3_q, z2_q, t, PACK + t) for t in tiles]
+        b = rows("b", 2 * S)
+        for t in tiles:
+            nc.scalar.activation(b[t][:, :S], b_acc[t][:], COPY)
+        late = keep.tile([P, 2, S], F32, name="hop_late", tag="z2_g", align_bytes=64)
+        hop.extend([late[:, 0, :], late[:, 1, :]])
+        fetch_hop(2)
+        fetch_hop(3)
+
         out_rows = out.rearrange("(p t) j -> p t j", t=PACK)
+        at6, at7, res = {}, {}, rows("res")
 
-        def finish_low(t):
-            nc.vector.tensor_tensor(low[t][:], hop[t][:], b6[t][:], ALU.min)
+        def fetch(t, dst, places):
+            dst[t] = row("at6" if dst is at6 else "at7", bufs=2)
+            if t < 2:
+                nc.vector.tensor_tensor(dst[t][:], b[t][:].indirect(places[:]), hop[t], ALU.subtract)
+            else:
+                nc.vector.tensor_copy(dst[t][:], b[t][:].indirect(places[:]))
 
-        def finish_out(t):
-            nc.vector.tensor_tensor(res[t][:], low[t][:], b7[t][:], ALU.max)
-            nc.sync.dma_start(out_rows[:, t, :], res[t][:])
+        def finish_turned(t):
+            step = row("step%d" % t)
+            nc.vector.scalar_tensor_tensor(step[:], at6[t][:], 0.0, at7[t][:], ALU.min, ALU.max)
+            turned = psum.tile([P, S], F32, name="turned", tag="bank%d" % t)
+            for c in range(0, S, P):
+                for term, first in ((hop[t], True), (step[:], False)):
+                    nc.tensor.matmul(turned[:, c : c + P], term[:, c : c + P], identity[:], start=first, stop=not first, is_transpose=True)
+            turned_sb = row("turned_sb%d" % t)
+            nc.scalar.activation(turned_sb[:], turned[:], COPY)
+            back = psum.tile([P, S], F32, name="back", tag="bank%d" % (2 + t))
+            for c in range(0, S, P):
+                nc.tensor.transpose(back[:, c : c + P], turned_sb[:, c : c + P], identity[:])
+            nc.scalar.activation(res[t][:], back[:], COPY)
+            nc.scalar.dma_start(out_rows[:, t, :], res[t][:])
 
-        for step in range(PACK + 2):
-            if step < PACK:
-                nc.vector.tensor_tensor(hop[step][:], a_half[step][:].indirect(n5_sb[:]), a[step][:], ALU.add)
-            if 0 <= step - 1 < PACK:
-                finish_low(step - 1)
-            if 0 <= step - 2 < PACK:
-                finish_out(step - 2)
+        low = {t: row("low%d" % t) for t in (2, 3)}
+
+        def take_min(t, places):
+            nc.vector.tensor_tensor(low[t][:, places], hop[t][:, places], at6[t][:, places], ALU.min)
+
+        def take_max(t, places):
+            nc.vector.tensor_tensor(res[t][:, places], low[t][:, places], at7[t][:, places], ALU.max)
+            nc.sync.dma_start(out_rows[:, t, places], res[t][:, places])
+
+        whole = slice(0, S)
+        fetch(0, at6, n6_sb)
+        fetch(0, at7, n7_sb)
+        fetch(1, at6, n6_sb)
+        fetch(1, at7, n7_sb)
+        finish_turned(0)
+        finish_turned(1)
+        fetch(2, at6, n6_sb)
+        fetch(2, at7, n7_sb)
+        take_min(2, whole)
+        fetch(3, at6, n6_sb)
+        take_max(2, whole)
+        fetch(3, at7, n7_sb)
+        for h in range(2):
+            take_min(3, halves[h])
+        for h in range(2):
+            take_max(3, halves[h])

from contextlib import ExitStack

import concourse.mybir as mybir
from concourse.masks import make_identity

K, T, S, N, H, W = 512, 2048, 512, 512, 512, 256
FLOPS = 2 * S * (K * H + 2 * H * N)

F32 = mybir.dt.float32
BF16 = mybir.dt.bfloat16
I32 = mybir.dt.int32
U32 = mybir.dt.uint32
U16 = mybir.dt.uint16
U8 = mybir.dt.uint8
FP8X4 = mybir.dt.float8_e4m3fn_x4
ALU = mybir.AluOpType
COPY = mybir.ActivationFunctionType.Copy

P = 128
PACK = 4
SCALAR_SHARE = 52


def tile_picked_forkclampbhopbond_none_p_kernel(
    tc, x_words, x_scales, w1, gn, w2, gm, w3, offs, n1, n2, n3, n4, n5, n6, n7, out
):
    nc = tc.nc
    tiles = range(PACK)

    with ExitStack() as ctx:
        keep = ctx.enter_context(tc.tile_pool(name="keep", bufs=1))
        psum = ctx.enter_context(tc.psum_pool(name="psum", bufs=1))

        def load_list(src, name):
            dst = keep.tile(list(src.shape), U16, name=name)
            nc.sync.dma_start(dst[:], src)
            return dst

        def load_weight(src, name):
            dst = keep.tile([P, PACK, src.shape[1]], F32, name=name)
            nc.sync.dma_start(dst[:], src.rearrange("(p j) c -> p j c", j=PACK))
            return dst

        def load_gain(src, name):
            dst = keep.tile([P, PACK], F32, name=name)
            nc.sync.dma_start(dst[:], src.rearrange("(p t) o -> p (t o)", t=PACK))
            return dst

        def dealt_views(raw, name):
            grouped = keep.tile([P, PACK, P, PACK], BF16, name=name, align_bytes=64)
            return grouped, grouped[:].rearrange("p t m j -> p m j t"), raw[:].rearrange("p j (m t) -> p m j t", t=PACK)

        def quantize(flat, name):
            codes = keep.tile([P, flat.shape[1] // PACK], U32, name=name + "_codes", align_bytes=64)
            scales = keep.tile([P, flat.shape[1] // PACK], U8, name=name + "_scales", align_bytes=64)
            nc.vector.quantize_mx(out=codes[:].bitcast(FP8X4), scales=scales[:], in_=flat)
            return codes, scales

        def product(weight, moving, t, bank, places=slice(0, S)):
            acc = psum.tile([P, places.stop - places.start], F32, name="acc", tag="bank%d" % bank)
            cols = slice(t * P, (t + 1) * P)
            nc.tensor.matmul_mx(
                out=acc[:],
                lhsT=weight[0][:, cols].bitcast(FP8X4),
                lhsT_scale=weight[1][:, cols],
                rhs=moving[0][:, places].bitcast(FP8X4),
                rhs_scale=moving[1][:, places],
                start=True,
                stop=True,
            )
            return acc

        def row(name, width=S, tag=None, bufs=1):
            return keep.tile([P, width], F32, name=name, tag=tag or name, bufs=bufs, align_bytes=64)

        def rows(name, width=S):
            return [row("%s%d" % (name, t), width) for t in tiles]

        table_scales = keep.tile([P, T], U8, name="table_scales")
        nc.vector.memset(table_scales[:].bitcast(I32), 0)
        offs_sb = load_list(offs, "offs_sb")
        w1_raw = load_weight(w1, "w1_raw")
        for q in range(4):
            nc.sync.dma_start(
                table_scales[32 * q : 32 * q + 4, :].bitcast(I32),
                x_scales[0, 4 * q : 4 * q + 4, :].bitcast(I32),
            )
        table_words = keep.tile([P, T], U32, name="table_words")
        nc.sync.dma_start(table_words[:].bitcast(I32), x_words[0].rearrange("p n t -> p (n t)").bitcast(I32))
        n3_sb = load_list(n3, "n3_sb")
        n4_sb = load_list(n4, "n4_sb")
        gn_sb = load_gain(gn, "gn_sb")
        n1_sb = load_list(n1, "n1_sb")
        n2_sb = load_list(n2, "n2_sb")
        w2_raw = load_weight(w2, "w2_raw")
        w3_raw = load_weight(w3, "w3_raw")
        gm_sb = load_gain(gm, "gm_sb")
        n5_sb = load_list(n5, "n5_sb")
        n6_sb = load_list(n6, "n6_sb")
        n7_sb = load_list(n7, "n7_sb")
        identity = keep.tile([P, P], F32, name="identity")
        make_identity(nc, identity[:])

        halves = [slice(0, S // 2), slice(S // 2, S)]
        list_halves = [slice(0, S // 32), slice(S // 32, S // 16)]

        x_scale_g = keep.tile([P, S], U8, name="x_scale_g", align_bytes=64)
        nc.vector.tensor_copy(x_scale_g[:], table_scales[:].indirect(offs_sb[:]))
        w1_g, dst, src = dealt_views(w1_raw, "w1_g")
        nc.scalar.activation(dst[:, :SCALAR_SHARE], src[:, :SCALAR_SHARE], COPY)
        nc.vector.tensor_copy(dst[:, SCALAR_SHARE:], src[:, SCALAR_SHARE:])
        w1_q = quantize(w1_g[:].rearrange("p t m j -> p (t m j)"), "w1")
        x_word_g = keep.tile([P, S], U32, name="x_word_g", tag="w1_g", align_bytes=64)
        for h in range(2):
            nc.vector.tensor_copy(x_word_g[:, halves[h]], table_words[:].indirect(offs_sb[:, list_halves[h]]))
        x_q = (x_word_g, x_scale_g)
        y_acc = [[(halves[h], product(w1_q, x_q, 0, PACK * h, halves[h])) for h in range(2)]]
        y_acc.extend([(slice(0, S), product(w1_q, x_q, t, t))] for t in range(1, PACK))
        y = rows("y")
        for t in tiles:
            for places, acc in y_acc[t]:
                nc.scalar.activation(y[t][:, places], acc[:], COPY)

        pa, pb = rows("pa", W), rows("pb", W)
        for t in tiles:
            nc.vector.tensor_copy(pa[t][:], y[t][:].indirect(n3_sb[:]))
            nc.vector.tensor_copy(pb[t][:], y[t][:].indirect(n4_sb[:]))

        gy, gy2 = rows("gy", 2 * S), rows("gy2")
        for t in tiles:
            for places, acc in y_acc[t]:
                nc.scalar.activation(gy[t][:, places], acc[:], COPY, scale=gn_sb[:, t : t + 1])
            nc.scalar.activation(gy2[t][:], gy[t][:, :S], COPY, scale=2.0)
        st, st_plain = rows("st", 2 * S), rows("st_plain")
        z = keep.tile([P, PACK, S], F32, name="z", align_bytes=64)
        for t in tiles:
            nc.vector.tensor_tensor(st[t][:, :S], gy[t][:].indirect(n1_sb[:]), gy2[t][:], ALU.add)
            nc.scalar.activation(st_plain[t][:], st[t][:, :S], COPY)
        for t in tiles:
            nc.vector.tensor_tensor(z[:, t, :], st[t][:].indirect(n2_sb[:]), st_plain[t][:], ALU.subtract)
        w2_g, dst, src = dealt_views(w2_raw, "w2_g")
        nc.scalar.activation(dst, src, COPY)
        w3_g, dst, src = dealt_views(w3_raw, "w3_g")
        nc.scalar.activation(dst, src, COPY)
        z_g = keep.tile([P, S, PACK], BF16, name="z_g", align_bytes=64)
        nc.scalar.activation(
            z_g[:].rearrange("p (c i) t -> p c t i", i=4),
            z[:].rearrange("p t (c i) -> p c t i", i=4),
            COPY,
            scale=-0.5,
        )

        z2_g = keep.tile([P, S, PACK], BF16, name="z2_g", align_bytes=64)

        def put_pairs(first, tags):
            pair = (first, first + 1)
            dt = {t: row("dt%d" % t, tag=tag) for t, tag in zip(pair, tags)}
            for places, op in ((n3_sb, ALU.add), (n4_sb, ALU.mult)):
                for t in pair:
                    nc.vector.tensor_tensor(dt[t][:].indirect(places[:]), pa[t][:], pb[t][:], op)
            for t in pair:
                nc.scalar.activation(z2_g[:, :, t], dt[t][:], COPY, scale=gm_sb[:, t : t + 1])

        put_pairs(0, ("st_plain2", "st_plain3"))
        w2_q = quantize(w2_g[:].rearrange("p t m j -> p (t m j)"), "w2")
        w3_q = quantize(w3_g[:].rearrange("p t m j -> p (t m j)"), "w3")
        z_q = quantize(z_g[:].rearrange("p s t -> p (s t)"), "z")
        a_acc = [product(w2_q, z_q, t, t) for t in tiles]
        a_half, a = rows("a_half", 2 * S), rows("a")

        def copy_a(t):
            nc.scalar.activation(a_half[t][:, :S], a_acc[t][:], COPY, scale=-0.5)
            nc.scalar.activation(a[t][:], a_acc[t][:], COPY)

        for t in range(PACK - 1):
            copy_a(t)
        put_pairs(2, ("z", "z_g"))
        copy_a(PACK - 1)

        early = keep.tile([P, 2, S], F32, name="hop_early")
        hop = [early[:, 0, :], early[:, 1, :]]

        def fetch_hop(t):
            nc.vector.tensor_tensor(hop[t], a_half[t][:].indirect(n5_sb[:]), a[t][:], ALU.add)

        fetch_hop(0)
        fetch_hop(1)
        z2_q = quantize(z2_g[:].rearrange("p s t -> p (s t)"), "z2")
        b_acc = [product(w3_q, z2_q, t, PACK + t) for t in tiles]
        b = rows("b", 2 * S)
        for t in tiles:
            nc.scalar.activation(b[t][:, :S], b_acc[t][:], COPY)
        late = keep.tile([P, 2, S], F32, name="hop_late", tag="z2_g", align_bytes=64)
        hop.extend([late[:, 0, :], late[:, 1, :]])
        fetch_hop(2)
        fetch_hop(3)

        out_rows = out.rearrange("(p t) j -> p t j", t=PACK)
        at6, at7, res = {}, {}, rows("res")

        def fetch(t, dst, places):
            dst[t] = row("at6" if dst is at6 else "at7", bufs=2)
            if t < 2:
                nc.vector.tensor_tensor(dst[t][:], b[t][:].indirect(places[:]), hop[t], ALU.subtract)
            else:
                nc.vector.tensor_copy(dst[t][:], b[t][:].indirect(places[:]))

        def finish_turned(t):
            step = row("step%d" % t)
            nc.vector.scalar_tensor_tensor(step[:], at6[t][:], 0.0, at7[t][:], ALU.min, ALU.max)
            turned = psum.tile([P, S], F32, name="turned", tag="bank%d" % t)
            for c in range(0, S, P):
                for term, first in ((hop[t], True), (step[:], False)):
                    nc.tensor.matmul(turned[:, c : c + P], term[:, c : c + P], identity[:], start=first, stop=not first, is_transpose=True)
            turned_sb = row("turned_sb%d" % t)
            nc.scalar.activation(turned_sb[:], turned[:], COPY)
            back = psum.tile([P, S], F32, name="back", tag="bank%d" % (2 + t))
            for c in range(0, S, P):
                nc.tensor.transpose(back[:, c : c + P], turned_sb[:, c : c + P], identity[:])
            nc.scalar.activation(res[t][:], back[:], COPY)
            nc.scalar.dma_start(out_rows[:, t, :], res[t][:])

        low = {t: row("low%d" % t) for t in (2, 3)}

        def take_min(t, places):
            nc.vector.tensor_tensor(low[t][:, places], hop[t][:, places], at6[t][:, places], ALU.min)

        def take_max(t, places):
            nc.vector.tensor_tensor(res[t][:, places], low[t][:, places], at7[t][:, places], ALU.max)
            nc.sync.dma_start(out_rows[:, t, places], res[t][:, places])

        whole = slice(0, S)
        fetch(0, at6, n6_sb)
        fetch(0, at7, n7_sb)
        fetch(1, at6, n6_sb)
        fetch(1, at7, n7_sb)
        finish_turned(0)
        finish_turned(1)
        fetch(2, at6, n6_sb)
        fetch(2, at7, n7_sb)
        take_min(2, whole)
        fetch(3, at6, n6_sb)
        take_max(2, whole)
        fetch(3, at7, n7_sb)
        for h in range(2):
            take_min(3, halves[h])
        for h in range(2):
            take_max(3, halves[h])
